import numpy as np
import ml_dtypes


def mxq(x, axis, fmt="e4m3"):
    dtype, down = {"e4m3": (ml_dtypes.float8_e4m3fn, 7), "e5m2": (ml_dtypes.float8_e5m2, 14)}[fmt]
    v = np.moveaxis(np.asarray(x, np.float32).astype(ml_dtypes.bfloat16).astype(np.float64), axis, -1)
    blocks = v.reshape(v.shape[:-1] + (-1, 32))
    amax = np.abs(blocks).max(-1, keepdims=True)
    byte = np.maximum(np.where(amax > 0, np.frexp(amax)[1] - 1 + 127, 0) - down, 1)
    scale = np.exp2(byte - 127.0)
    codes = (blocks / scale).astype(np.float32).astype(dtype).astype(np.float64)
    return np.moveaxis((codes * scale).reshape(v.shape), -1, axis)


WIDE = False


def mx_kscale(k):
    if not WIDE:
        return np.ones(k)
    levels = np.array([10, -10, 5, -5, 0])
    if k % 512:
        return np.exp2(np.random.permutation(np.resize(levels, k // 32))).repeat(32)
    a = np.empty((k // 512, 16))
    for p in range(k // 512):
        a[p, :8] = np.random.permutation(np.resize(levels, 8))
        for g in range(8):
            far = levels[np.abs(levels - a[p, g]) >= 10]
            a[p, g + 8] = far[np.random.randint(len(far))]
    return np.exp2(a.ravel()).repeat(32)


def f64(x):
    return np.asarray(x).astype(np.float64)


def striped(idx):
    return np.tile(idx.reshape(-1, 16).T, (8, 1)).astype(np.uint16)


def unstriped(offs):
    return offs[:16].T.reshape(-1).astype(np.int64)


def pack_weight(w):
    k, n = w.shape
    w = f64(np.asarray(w, np.float32).astype(ml_dtypes.bfloat16)).reshape(k // 32, 32, n)
    amax = np.abs(w).max(1)
    byte = np.clip(np.where(amax > 0, np.frexp(amax)[1] - 1 + 127 - 7, 1), 1, 254)
    scaled = (w * np.exp2(127.0 - byte)[:, None, :]).reshape(k, n).astype(np.float32)
    words = np.ascontiguousarray(scaled.reshape(k // 512, 128, 4, n).transpose(0, 1, 3, 2)).astype(ml_dtypes.float8_e4m3fn).view(np.uint8)
    return words, np.ascontiguousarray(byte.astype(np.uint8).reshape(k // 512, 16, n))


def unpack_weight(words, scales):
    g, p, n, _ = words.shape
    vals = np.ascontiguousarray(words).view(ml_dtypes.float8_e4m3fn).astype(np.float64) * np.repeat(np.exp2(scales.astype(np.float64) - 127.0), 8, axis=1)[..., None]
    return vals.transpose(0, 1, 3, 2).reshape(g * 512, n)


K, T, S, V = 1024, 2048, 512, 512
P = 2 ** 7


def setup_inputs():
    n = np.random.standard_normal
    s = mx_kscale(K)[:, None]
    packed_xT = pack_weight(n((K, T)) * s)
    return {
        "x_words": packed_xT[0],
        "x_scales": packed_xT[1],
        "hT": (n((K, V)) / np.sqrt(K) / s).astype(np.float32),
        "bias": (np.tile(0.5 * n(T), (P, 1))).astype(np.float32),
        "isa": (np.tile((np.random.uniform(size=S) < 0.3) * 1.0, (P, 1))).astype(np.float32),
        "thr": (-5.0 + 0.7 * n((V, 1))).astype(np.float32),
        "offs": striped(np.random.permutation(T)[:S]),
    }


def reference(x_words, x_scales, hT, bias, isa, thr, offs):
    hTq = mxq(f64(hT), 0, "e4m3")
    xq = unpack_weight(x_words, x_scales)[:, unstriped(offs)]
    y = 0.8 * (hTq.T @ xq) + f64(bias)[:1][:, unstriped(offs)]
    mar = y + f64(thr)
    ex = np.exp(mar)
    ep = ex * f64(isa)[:1]
    tp = ep.sum(axis=1, keepdims=True)
    lzp = np.log(tp + 1.0)
    en = ex * (-1.0 * f64(isa)[:1] + 1.0)
    tn = en.sum(axis=1, keepdims=True)
    lzn = np.log(tn + 1.0)
    return 20.0 * (f64(isa)[:1] * np.exp(mar - lzp)) - (20.0 * ((-1.0 * f64(isa)[:1] + 1.0) * np.exp(mar - lzn)))

@@ -1,0 +1,199 @@
+from contextlib import ExitStack
+
+import concourse.mybir as mybir
+from concourse.masks import make_identity
+
+K, T, S, V = 1024, 2048, 512, 512
+FLOPS = 2 * K * S * V
+
+F32 = mybir.dt.float32
+BF16 = mybir.dt.bfloat16
+I32 = mybir.dt.int32
+U32 = mybir.dt.uint32
+U16 = mybir.dt.uint16
+U8 = mybir.dt.uint8
+FP8X4 = mybir.dt.float8_e4m3fn_x4
+ALU = mybir.AluOpType
+ACT = mybir.ActivationFunctionType
+
+P = 128
+PACK = 4
+K_PASS = P * PACK
+PASSES = K // K_PASS
+BLOCKS = V // P
+LAST = P - 1
+BIAS_ROWS = slice(104, 120)
+ISA_ROWS = slice(120, 124)
+THR_ROWS = slice(124, 128)
+
+
+def tile_picked_yatlop_prob_p_kernel(tc, x_words, x_scales, hT, bias, isa, thr, offs, out):
+    nc = tc.nc
+    with ExitStack() as ctx:
+        keep = ctx.enter_context(tc.tile_pool(name="keep", bufs=1))
+        late = ctx.enter_context(tc.tile_pool(name="late", bufs=1))
+        work = ctx.enter_context(tc.tile_pool(name="work", bufs=2))
+        psum = ctx.enter_context(tc.psum_pool(name="psum", bufs=1))
+
+        def place(name, shape, dtype, offset):
+            return late.tile(shape, dtype, name=name, offset=offset, align_bytes=64)
+
+        offsets = keep.tile([P, S // 16], U16, name="offsets")
+        nc.sync.dma_start(offsets[:], offs)
+
+        scale_table = place("scale_table", [P, T], U8, 36864)
+        nc.vector.memset(scale_table[:].bitcast(I32), 0)
+        bias_table = place("bias_table", [P, T], F32, 0)
+        nc.sync.dma_start(out=bias_table[LAST:P, :], in_=bias[0:1, :])
+        rows = place("rows", [P, P], F32, 24576 - 256)
+        nc.scalar.dma_start(out=rows[BIAS_ROWS, :], in_=bias[0:1, :].rearrange("o (b p) -> (o b) p", p=P))
+        nc.scalar.dma_start(out=rows[ISA_ROWS, :], in_=isa[0:1, :].rearrange("o (b p) -> (o b) p", p=P))
+        nc.sync.dma_start(out=rows[THR_ROWS, :], in_=thr.rearrange("(b p) o -> b (p o)", p=P))
+        ident = keep.tile([P, P], F32, name="ident")
+        make_identity(nc, ident[:])
+        nc.gpsimd.memset(rows[0 : BIAS_ROWS.start, :], 0.0)
+        nc.vector.memset(bias_table[0:LAST, :], 0.0)
+
+        def load_words(o, table):
+            nc.sync.dma_start(out=table[:], in_=x_words[o].rearrange("p n t -> p (n t)").bitcast(I32))
+
+        raws = {}
+
+        def load_h(flat, o, b0, b1):
+            dst = flat.rearrange("p (j w) -> p j w", j=PACK)
+            nc.sync.dma_start(
+                out=dst,
+                in_=hT[o * K_PASS : (o + 1) * K_PASS, b0 * P : b1 * P].rearrange("(p j) w -> p j w", j=PACK),
+            )
+            for b in range(b0, b1):
+                raws[b, o] = dst[:, :, (b - b0) * P : (b - b0 + 1) * P]
+
+        word_table0 = place("word_table0", [P, T], I32, 8192)
+        load_words(0, word_table0)
+        for o in range(PASSES):
+            raw = place(f"raw0_{o}", [P, K_PASS], F32, 43008 + 2048 * o)
+            load_h(raw[:], o, 0, 1)
+        for q in range(4):
+            nc.sync.dma_start(
+                out=scale_table[32 * q : 32 * q + 8, :].bitcast(I32),
+                in_=x_scales[:, 4 * q : 4 * q + 4, :].bitcast(I32),
+            )
+
+        cols_ps = psum.tile([P, P], F32, name="cols_ps", tag="acc3")
+        nc.tensor.transpose(cols_ps[:], rows[:], ident[:])
+        word_table1 = place("word_table1", [P, T], I32, 16384)
+        load_words(1, word_table1)
+        rest = place("rest", [P, 6 * K_PASS], F32, 24576)
+        for b in range(1, BLOCKS):
+            for o in range(PASSES):
+                start = (PASSES * (b - 1) + o) * K_PASS
+                load_h(rest[:, start : start + K_PASS], o, b, b + 1)
+
+
+        lane_top = keep.tile([P, 1], F32, name="lane_top")
+        nc.vector.tensor_reduce(lane_top[:], cols_ps[:, BIAS_ROWS], mybir.AxisListType.X, ALU.max)
+        isa_cols = keep.tile([P, BLOCKS], F32, name="isa_cols")
+        nc.vector.tensor_copy(isa_cols[:], cols_ps[:, ISA_ROWS])
+        top_ps = psum.tile([P, P], F32, name="top_ps")
+        nc.tensor.transpose(top_ps[:], lane_top[:].to_broadcast([P, P]), ident[:])
+        neg_top = keep.tile([P, 1], F32, name="neg_top")
+        nc.vector.tensor_reduce(neg_top[:], top_ps[:], mybir.AxisListType.X, ALU.max, negate=True)
+        shift = keep.tile([P, BLOCKS], F32, name="shift")
+        nc.vector.tensor_scalar(shift[:], cols_ps[:, THR_ROWS], neg_top[:], None, ALU.subtract)
+        picked_bias = keep.tile([P, S], F32, name="picked_bias")
+        nc.vector.tensor_copy(picked_bias[:], bias_table[:].indirect(offsets[:]))
+        bias_ps = psum.tile([P, BLOCKS, P], F32, name="bias_ps")
+        for b in range(BLOCKS):
+            nc.tensor.transpose(bias_ps[:, b, :], picked_bias[:, b * P : (b + 1) * P], ident[:])
+
+        codes = {}
+        scales = {}
+        grouped = {}
+
+        def interleave(b, copy):
+            grouped[b] = place(f"grouped{b}", [P, PASSES, P, PACK], BF16, (38912, 16384, 45056, 18432)[b])
+            for o in range(PASSES):
+                copy(
+                    grouped[b][:, o].rearrange("p (c i) t -> p c t i", i=4),
+                    raws[b, o].rearrange("p t (c i) -> p c t i", i=4),
+                )
+
+        def quantize(b):
+            codes[b] = place(f"codes{b}", [P, PASSES, P], U32, (45056, 18432, 12288, 13312)[b])
+            scales[b] = keep.tile([P, PASSES, P], U8, name=f"scales{b}", align_bytes=64)
+            nc.vector.quantize_mx(
+                out=codes[b][:].rearrange("p o w -> p (o w)").bitcast(FP8X4),
+                scales=scales[b][:].rearrange("p o w -> p (o w)"),
+                in_=grouped[b][:].rearrange("p o w j -> p (o w j)"),
+            )
+
+        def prepare(b, copy):
+            interleave(b, copy)
+            quantize(b)
+
+        picked_words = [place("picked_words0", [P, S], U32, 0)]
+        nc.vector.tensor_copy(picked_words[0][:], word_table0[:].bitcast(U32).indirect(offsets[:]))
+
+        picked_scales = place("picked_scales", [P, S], U8, 8192)
+        nc.vector.tensor_copy(picked_scales[:], scale_table[:].indirect(offsets[:]))
+
+        interleave(0, nc.scalar.copy)
+        weight_all = place("weight_all", [P, BLOCKS], F32, 45056)
+        nc.scalar.activation(weight_all[:], bias_ps[:, :, LAST], ACT.Exp, bias=neg_top[:])
+        weight_cols = place("weight_cols", [P, 2, BLOCKS], F32, 8192 + 512)
+        nc.vector.tensor_tensor(weight_cols[:, 0, :], weight_all[:], isa_cols[:], ALU.mult)
+        nc.vector.tensor_tensor(weight_cols[:, 1, :], weight_all[:], weight_cols[:, 0, :], ALU.subtract)
+        weights = []
+        for g in range(2):
+            spread = psum.tile([P, S], F32, name=f"weights{g}")
+            for b in range(BLOCKS):
+                nc.tensor.transpose(
+                    spread[:, b * P : (b + 1) * P], weight_cols[:, g, b : b + 1].to_broadcast([P, P]), ident[:]
+                )
+            weights.append(spread)
+
+        def finish(b, pieces):
+            acc = psum.tile([P, S], F32, name=f"acc{b}")
+            for o in range(PASSES):
+                nc.tensor.matmul_mx(
+                    out=acc[:],
+                    lhsT=codes[b][:, o].bitcast(FP8X4),
+                    lhsT_scale=scales[b][:, o],
+                    rhs=picked_words[o][:].bitcast(FP8X4),
+                    rhs_scale=picked_scales[4 * o : P, :],
+                    start=(o == 0),
+                    stop=(o == PASSES - 1),
+                )
+            base = work.tile([P, S], F32, name="base")
+            nc.scalar.activation(base[:], acc[:], ACT.Exp, bias=shift[:, b : b + 1], scale=0.8)
+            ex = work.tile([P, 2, S], F32, name="ex")
+            total = work.tile([P, 2], F32, name="total")
+            for g in range(2):
+                nc.vector.scalar_tensor_tensor(
+                    ex[:, g], weights[g][:], 1.0, base[:], ALU.mult, ALU.mult, accum_out=total[:, g : g + 1]
+                )
+            denom = work.tile([P, 2], F32, name="denom")
+            nc.vector.tensor_scalar(denom[:], total[:], 1.0, 0.05, ALU.add, ALU.mult)
+            factor = work.tile([P, 2], F32, name="factor")
+            nc.vector.reciprocal(factor[:], denom[:])
+            other = work.tile([P, S], F32, name="other")
+            result = keep.tile([P, S], F32, name=f"result{b}")
+            width = S // pieces
+            for c in range(0, S, width):
+                cols = slice(c, c + width)
+                nc.scalar.activation(other[:, cols], ex[:, 1, cols], ACT.Copy, scale=factor[:, 1:2])
+                nc.vector.scalar_tensor_tensor(
+                    result[:, cols], ex[:, 0, cols], factor[:, 0:1], other[:, cols], ALU.mult, ALU.subtract
+                )
+                nc.sync.dma_start(out=out[b * P : (b + 1) * P, cols], in_=result[:, cols])
+
+        quantize(0)
+        picked_words.append(place("picked_words1", [P, S], U32, 37888))
+        nc.vector.tensor_copy(picked_words[1][:], word_table1[:].bitcast(U32).indirect(offsets[:]))
+        prepare(1, nc.vector.tensor_copy)
+        finish(0, 1)
+        prepare(2, nc.scalar.copy)
+        finish(1, 1)
+        prepare(3, nc.scalar.copy)
+        finish(2, 1)
+        finish(3, 2)

@@ -22,7 +22,6 @@ K_PASS = P * PACK
 PASSES = K // K_PASS
 BLOCKS = V // P
 LAST = P - 1
-BIAS_ROWS = slice(104, 120)
 ISA_ROWS = slice(120, 124)
 THR_ROWS = slice(124, 128)
 
@@ -32,7 +31,7 @@ def tile_picked_yatlop_prob_p_kernel(tc, x_words, x_scales, hT, bias, isa, thr, 
     with ExitStack() as ctx:
         keep = ctx.enter_context(tc.tile_pool(name="keep", bufs=1))
         late = ctx.enter_context(tc.tile_pool(name="late", bufs=1))
-        work = ctx.enter_context(tc.tile_pool(name="work", bufs=2))
+        work = ctx.enter_context(tc.tile_pool(name="work", bufs=4))
         psum = ctx.enter_context(tc.psum_pool(name="psum", bufs=1))
 
         def place(name, shape, dtype, offset):
@@ -46,12 +45,11 @@ def tile_picked_yatlop_prob_p_kernel(tc, x_words, x_scales, hT, bias, isa, thr, 
         bias_table = place("bias_table", [P, T], F32, 0)
         nc.sync.dma_start(out=bias_table[LAST:P, :], in_=bias[0:1, :])
         rows = place("rows", [P, P], F32, 24576 - 256)
-        nc.scalar.dma_start(out=rows[BIAS_ROWS, :], in_=bias[0:1, :].rearrange("o (b p) -> (o b) p", p=P))
         nc.scalar.dma_start(out=rows[ISA_ROWS, :], in_=isa[0:1, :].rearrange("o (b p) -> (o b) p", p=P))
-        nc.sync.dma_start(out=rows[THR_ROWS, :], in_=thr.rearrange("(b p) o -> b (p o)", p=P))
+        nc.scalar.dma_start(out=rows[THR_ROWS, :], in_=thr.rearrange("(b p) o -> b (p o)", p=P))
         ident = keep.tile([P, P], F32, name="ident")
         make_identity(nc, ident[:])
-        nc.gpsimd.memset(rows[0 : BIAS_ROWS.start, :], 0.0)
+        nc.gpsimd.memset(rows[0 : ISA_ROWS.start, :], 0.0)
         nc.vector.memset(bias_table[0:LAST, :], 0.0)
 
         def load_words(o, table):
@@ -90,28 +88,29 @@ def tile_picked_yatlop_prob_p_kernel(tc, x_words, x_scales, hT, bias, isa, thr, 
                 load_h(rest[:, start : start + K_PASS], o, b, b + 1)
 
 
-        lane_top = keep.tile([P, 1], F32, name="lane_top")
-        nc.vector.tensor_reduce(lane_top[:], cols_ps[:, BIAS_ROWS], mybir.AxisListType.X, ALU.max)
-        isa_cols = keep.tile([P, BLOCKS], F32, name="isa_cols")
-        nc.vector.tensor_copy(isa_cols[:], cols_ps[:, ISA_ROWS])
-        top_ps = psum.tile([P, P], F32, name="top_ps")
-        nc.tensor.transpose(top_ps[:], lane_top[:].to_broadcast([P, P]), ident[:])
-        neg_top = keep.tile([P, 1], F32, name="neg_top")
-        nc.vector.tensor_reduce(neg_top[:], top_ps[:], mybir.AxisListType.X, ALU.max, negate=True)
-        shift = keep.tile([P, BLOCKS], F32, name="shift")
-        nc.vector.tensor_scalar(shift[:], cols_ps[:, THR_ROWS], neg_top[:], None, ALU.subtract)
-        picked_bias = keep.tile([P, S], F32, name="picked_bias")
+        sides = place("sides", [P, BLOCKS], F32, 47040)
+        nc.scalar.activation(sides[:], cols_ps[:, ISA_ROWS], ACT.Copy, bias=-20.0, scale=40.0)
+        ones = keep.tile([P, 2], F32, name="ones")
+        nc.gpsimd.memset(ones[:, 0:1], 1.0)
+        nc.gpsimd.memset(ones[:, 1:2], -1.0)
+        picked_bias = place("picked_bias", [P, S], F32, 47104)
         nc.vector.tensor_copy(picked_bias[:], bias_table[:].indirect(offsets[:]))
-        bias_ps = psum.tile([P, BLOCKS, P], F32, name="bias_ps")
+        neg_top = keep.tile([P, 1], F32, name="neg_top")
+        nc.vector.tensor_reduce(neg_top[:], picked_bias[:], mybir.AxisListType.X, ALU.max, negate=True)
+        weight_row = keep.tile([P, S], F32, name="weight_row")
+        nc.scalar.activation(weight_row[:], picked_bias[:], ACT.Exp, bias=neg_top[:])
+        top_ps = psum.tile([P, P], F32, name="top_ps")
+        nc.tensor.transpose(top_ps[:], neg_top[:].to_broadcast([P, P]), ident[:])
+        weight_ps = psum.tile([P, BLOCKS, P], F32, name="weight_ps")
         for b in range(BLOCKS):
-            nc.tensor.transpose(bias_ps[:, b, :], picked_bias[:, b * P : (b + 1) * P], ident[:])
+            nc.tensor.transpose(weight_ps[:, b, :], weight_row[:, b * P : (b + 1) * P], ident[:])
 
         codes = {}
         scales = {}
         grouped = {}
 
         def interleave(b, copy):
-            grouped[b] = place(f"grouped{b}", [P, PASSES, P, PACK], BF16, (38912, 16384, 45056, 18432)[b])
+            grouped[b] = place(f"grouped{b}", [P, PASSES, P, PACK], BF16, (47104, 16384, 36992, 18432)[b])
             for o in range(PASSES):
                 copy(
                     grouped[b][:, o].rearrange("p (c i) t -> p c t i", i=4),
@@ -119,7 +118,7 @@ def tile_picked_yatlop_prob_p_kernel(tc, x_words, x_scales, hT, bias, isa, thr, 
                 )
 
         def quantize(b):
-            codes[b] = place(f"codes{b}", [P, PASSES, P], U32, (45056, 18432, 12288, 13312)[b])
+            codes[b] = place(f"codes{b}", [P, PASSES, P], U32, (36992, 18432, 12288, 13312)[b])
             scales[b] = keep.tile([P, PASSES, P], U8, name=f"scales{b}", align_bytes=64)
             nc.vector.quantize_mx(
                 out=codes[b][:].rearrange("p o w -> p (o w)").bitcast(FP8X4),
@@ -136,21 +135,15 @@ def tile_picked_yatlop_prob_p_kernel(tc, x_words, x_scales, hT, bias, isa, thr, 
 
         picked_scales = place("picked_scales", [P, S], U8, 8192)
         nc.vector.tensor_copy(picked_scales[:], scale_table[:].indirect(offsets[:]))
-
         interleave(0, nc.scalar.copy)
-        weight_all = place("weight_all", [P, BLOCKS], F32, 45056)
-        nc.scalar.activation(weight_all[:], bias_ps[:, :, LAST], ACT.Exp, bias=neg_top[:])
-        weight_cols = place("weight_cols", [P, 2, BLOCKS], F32, 8192 + 512)
-        nc.vector.tensor_tensor(weight_cols[:, 0, :], weight_all[:], isa_cols[:], ALU.mult)
-        nc.vector.tensor_tensor(weight_cols[:, 1, :], weight_all[:], weight_cols[:, 0, :], ALU.subtract)
-        weights = []
-        for g in range(2):
-            spread = psum.tile([P, S], F32, name=f"weights{g}")
-            for b in range(BLOCKS):
-                nc.tensor.transpose(
-                    spread[:, b * P : (b + 1) * P], weight_cols[:, g, b : b + 1].to_broadcast([P, P]), ident[:]
-                )
-            weights.append(spread)
+        weight_cols = place("weight_cols", [P, BLOCKS], F32, 36864)
+        nc.vector.tensor_tensor(weight_cols[:], weight_ps[:, :, LAST], sides[:], ALU.mult)
+        shift = place("shift", [P, BLOCKS], F32, 36864 + 64)
+        nc.vector.tensor_scalar(shift[:], cols_ps[:, THR_ROWS], top_ps[:, LAST:P], None, ALU.subtract)
+        weights = psum.tile([P, S], F32, name="weights")
+        for b in range(BLOCKS):
+            nc.tensor.transpose(weights[:, b * P : (b + 1) * P], weight_cols[:, b : b + 1].to_broadcast([P, P]), ident[:])
+
 
         def finish(b, pieces):
             acc = psum.tile([P, S], F32, name=f"acc{b}")
@@ -168,12 +161,12 @@ def tile_picked_yatlop_prob_p_kernel(tc, x_words, x_scales, hT, bias, isa, thr, 
             nc.scalar.activation(base[:], acc[:], ACT.Exp, bias=shift[:, b : b + 1], scale=0.8)
             ex = work.tile([P, 2, S], F32, name="ex")
             total = work.tile([P, 2], F32, name="total")
-            for g in range(2):
-                nc.vector.scalar_tensor_tensor(
-                    ex[:, g], weights[g][:], 1.0, base[:], ALU.mult, ALU.mult, accum_out=total[:, g : g + 1]
-                )
             denom = work.tile([P, 2], F32, name="denom")
-            nc.vector.tensor_scalar(denom[:], total[:], 1.0, 0.05, ALU.add, ALU.mult)
+            for g, side in enumerate((ALU.max, ALU.min)):
+                nc.vector.scalar_tensor_tensor(
+                    ex[:, g], weights[:], 0.0, base[:], side, ALU.mult, accum_out=total[:, g : g + 1]
+                )
+            nc.vector.scalar_tensor_tensor(denom[:], total[:], 0.05, ones[:], ALU.mult, ALU.add)
             factor = work.tile([P, 2], F32, name="factor")
             nc.vector.reciprocal(factor[:], denom[:])
             other = work.tile([P, S], F32, name="other")
@@ -188,7 +181,7 @@ def tile_picked_yatlop_prob_p_kernel(tc, x_words, x_scales, hT, bias, isa, thr, 
                 nc.sync.dma_start(out=out[b * P : (b + 1) * P, cols], in_=result[:, cols])
 
         quantize(0)
-        picked_words.append(place("picked_words1", [P, S], U32, 37888))
+        picked_words.append(place("picked_words1", [P, S], U32, 47040))
         nc.vector.tensor_copy(picked_words[1][:], word_table1[:].bitcast(U32).indirect(offsets[:]))
         prepare(1, nc.vector.tensor_copy)
         finish(0, 1)

@@ -69,7 +69,7 @@ def tile_picked_yatlop_prob_p_kernel(tc, x_words, x_scales, hT, bias, isa, thr, 
         word_table0 = place("word_table0", [P, T], I32, 8192)
         load_words(0, word_table0)
         for o in range(PASSES):
-            raw = place(f"raw0_{o}", [P, K_PASS], F32, 43008 + 2048 * o)
+            raw = place(f"raw0_{o}", [P, K_PASS], F32, 40960 + 2048 * o)
             load_h(raw[:], o, 0, 1)
         for q in range(4):
             nc.sync.dma_start(
@@ -126,6 +126,9 @@ def tile_picked_yatlop_prob_p_kernel(tc, x_words, x_scales, hT, bias, isa, thr, 
                 in_=grouped[b][:].rearrange("p o w j -> p (o w j)"),
             )
 
+        def gpsimd_copy(dst, src):
+            nc.gpsimd.tensor_scalar(dst, src, 1.0, 0.0, ALU.mult, ALU.add)
+
         def prepare(b, copy):
             interleave(b, copy)
             quantize(b)
@@ -162,11 +165,20 @@ def tile_picked_yatlop_prob_p_kernel(tc, x_words, x_scales, hT, bias, isa, thr, 
             ex = work.tile([P, 2, S], F32, name="ex")
             total = work.tile([P, 2], F32, name="total")
             denom = work.tile([P, 2], F32, name="denom")
-            for g, side in enumerate((ALU.max, ALU.min)):
-                nc.vector.scalar_tensor_tensor(
-                    ex[:, g], weights[:], 0.0, base[:], side, ALU.mult, accum_out=total[:, g : g + 1]
-                )
-            nc.vector.scalar_tensor_tensor(denom[:], total[:], 0.05, ones[:], ALU.mult, ALU.add)
+            if b == 1:
+                signed = work.tile([P, S], F32, name="signed")
+                nc.vector.tensor_tensor(signed[:], weights[:], base[:], ALU.mult)
+                for g in range(2):
+                    nc.scalar.activation(
+                        ex[:, g], signed[:], ACT.Relu, scale=1.0 - 2.0 * g, accum_out=total[:, g : g + 1]
+                    )
+                nc.vector.tensor_scalar(denom[:], total[:], 0.05, 1.0, ALU.mult, ALU.add)
+            else:
+                for g, side in enumerate((ALU.max, ALU.min)):
+                    nc.vector.scalar_tensor_tensor(
+                        ex[:, g], weights[:], 0.0, base[:], side, ALU.mult, accum_out=total[:, g : g + 1]
+                    )
+                nc.vector.scalar_tensor_tensor(denom[:], total[:], 0.05, ones[:], ALU.mult, ALU.add)
             factor = work.tile([P, 2], F32, name="factor")
             nc.vector.reciprocal(factor[:], denom[:])
             other = work.tile([P, S], F32, name="other")
@@ -185,8 +197,8 @@ def tile_picked_yatlop_prob_p_kernel(tc, x_words, x_scales, hT, bias, isa, thr, 
         nc.vector.tensor_copy(picked_words[1][:], word_table1[:].bitcast(U32).indirect(offsets[:]))
         prepare(1, nc.vector.tensor_copy)
         finish(0, 1)
-        prepare(2, nc.scalar.copy)
+        prepare(2, gpsimd_copy)
         finish(1, 1)
-        prepare(3, nc.scalar.copy)
+        prepare(3, gpsimd_copy)
         finish(2, 1)
         finish(3, 2)

from contextlib import ExitStack

import concourse.mybir as mybir
from concourse.masks import make_identity

K, T, S, V = 1024, 2048, 512, 512
FLOPS = 2 * K * S * V

F32 = mybir.dt.float32
BF16 = mybir.dt.bfloat16
I32 = mybir.dt.int32
U32 = mybir.dt.uint32
U16 = mybir.dt.uint16
U8 = mybir.dt.uint8
FP8X4 = mybir.dt.float8_e4m3fn_x4
ALU = mybir.AluOpType
ACT = mybir.ActivationFunctionType

P = 128
PACK = 4
K_PASS = P * PACK
PASSES = K // K_PASS
BLOCKS = V // P
LAST = P - 1
ISA_ROWS = slice(120, 124)
THR_ROWS = slice(124, 128)


def tile_picked_yatlop_prob_p_kernel(tc, x_words, x_scales, hT, bias, isa, thr, offs, out):
    nc = tc.nc
    with ExitStack() as ctx:
        keep = ctx.enter_context(tc.tile_pool(name="keep", bufs=1))
        late = ctx.enter_context(tc.tile_pool(name="late", bufs=1))
        work = ctx.enter_context(tc.tile_pool(name="work", bufs=4))
        psum = ctx.enter_context(tc.psum_pool(name="psum", bufs=1))

        def place(name, shape, dtype, offset):
            return late.tile(shape, dtype, name=name, offset=offset, align_bytes=64)

        offsets = keep.tile([P, S // 16], U16, name="offsets")
        nc.sync.dma_start(offsets[:], offs)

        scale_table = place("scale_table", [P, T], U8, 36864)
        nc.vector.memset(scale_table[:].bitcast(I32), 0)
        bias_table = place("bias_table", [P, T], F32, 0)
        nc.sync.dma_start(out=bias_table[LAST:P, :], in_=bias[0:1, :])
        rows = place("rows", [P, P], F32, 24576 - 256)
        nc.scalar.dma_start(out=rows[ISA_ROWS, :], in_=isa[0:1, :].rearrange("o (b p) -> (o b) p", p=P))
        nc.scalar.dma_start(out=rows[THR_ROWS, :], in_=thr.rearrange("(b p) o -> b (p o)", p=P))
        ident = keep.tile([P, P], F32, name="ident")
        make_identity(nc, ident[:])
        nc.gpsimd.memset(rows[0 : ISA_ROWS.start, :], 0.0)
        nc.vector.memset(bias_table[0:LAST, :], 0.0)

        def load_words(o, table):
            nc.sync.dma_start(out=table[:], in_=x_words[o].rearrange("p n t -> p (n t)").bitcast(I32))

        raws = {}

        def load_h(flat, o, b0, b1):
            dst = flat.rearrange("p (j w) -> p j w", j=PACK)
            nc.sync.dma_start(
                out=dst,
                in_=hT[o * K_PASS : (o + 1) * K_PASS, b0 * P : b1 * P].rearrange("(p j) w -> p j w", j=PACK),
            )
            for b in range(b0, b1):
                raws[b, o] = dst[:, :, (b - b0) * P : (b - b0 + 1) * P]

        word_table0 = place("word_table0", [P, T], I32, 8192)
        load_words(0, word_table0)
        for o in range(PASSES):
            raw = place(f"raw0_{o}", [P, K_PASS], F32, 40960 + 2048 * o)
            load_h(raw[:], o, 0, 1)
        for q in range(4):
            nc.sync.dma_start(
                out=scale_table[32 * q : 32 * q + 8, :].bitcast(I32),
                in_=x_scales[:, 4 * q : 4 * q + 4, :].bitcast(I32),
            )

        cols_ps = psum.tile([P, P], F32, name="cols_ps", tag="acc3")
        nc.tensor.transpose(cols_ps[:], rows[:], ident[:])
        word_table1 = place("word_table1", [P, T], I32, 16384)
        load_words(1, word_table1)
        rest = place("rest", [P, 6 * K_PASS], F32, 24576)
        for b in range(1, BLOCKS):
            for o in range(PASSES):
                start = (PASSES * (b - 1) + o) * K_PASS
                load_h(rest[:, start : start + K_PASS], o, b, b + 1)


        sides = place("sides", [P, BLOCKS], F32, 47040)
        nc.scalar.activation(sides[:], cols_ps[:, ISA_ROWS], ACT.Copy, bias=-20.0, scale=40.0)
        ones = keep.tile([P, 2], F32, name="ones")
        nc.gpsimd.memset(ones[:, 0:1], 1.0)
        nc.gpsimd.memset(ones[:, 1:2], -1.0)
        picked_bias = place("picked_bias", [P, S], F32, 47104)
        nc.vector.tensor_copy(picked_bias[:], bias_table[:].indirect(offsets[:]))
        neg_top = keep.tile([P, 1], F32, name="neg_top")
        nc.vector.tensor_reduce(neg_top[:], picked_bias[:], mybir.AxisListType.X, ALU.max, negate=True)
        weight_row = keep.tile([P, S], F32, name="weight_row")
        nc.scalar.activation(weight_row[:], picked_bias[:], ACT.Exp, bias=neg_top[:])
        top_ps = psum.tile([P, P], F32, name="top_ps")
        nc.tensor.transpose(top_ps[:], neg_top[:].to_broadcast([P, P]), ident[:])
        weight_ps = psum.tile([P, BLOCKS, P], F32, name="weight_ps")
        for b in range(BLOCKS):
            nc.tensor.transpose(weight_ps[:, b, :], weight_row[:, b * P : (b + 1) * P], ident[:])

        codes = {}
        scales = {}
        grouped = {}

        def interleave(b, copy):
            grouped[b] = place(f"grouped{b}", [P, PASSES, P, PACK], BF16, (47104, 16384, 36992, 18432)[b])
            for o in range(PASSES):
                copy(
                    grouped[b][:, o].rearrange("p (c i) t -> p c t i", i=4),
                    raws[b, o].rearrange("p t (c i) -> p c t i", i=4),
                )

        def quantize(b):
            codes[b] = place(f"codes{b}", [P, PASSES, P], U32, (36992, 18432, 12288, 13312)[b])
            scales[b] = keep.tile([P, PASSES, P], U8, name=f"scales{b}", align_bytes=64)
            nc.vector.quantize_mx(
                out=codes[b][:].rearrange("p o w -> p (o w)").bitcast(FP8X4),
                scales=scales[b][:].rearrange("p o w -> p (o w)"),
                in_=grouped[b][:].rearrange("p o w j -> p (o w j)"),
            )

        def gpsimd_copy(dst, src):
            nc.gpsimd.tensor_scalar(dst, src, 1.0, 0.0, ALU.mult, ALU.add)

        def prepare(b, copy):
            interleave(b, copy)
            quantize(b)

        picked_words = [place("picked_words0", [P, S], U32, 0)]
        nc.vector.tensor_copy(picked_words[0][:], word_table0[:].bitcast(U32).indirect(offsets[:]))

        picked_scales = place("picked_scales", [P, S], U8, 8192)
        nc.vector.tensor_copy(picked_scales[:], scale_table[:].indirect(offsets[:]))
        interleave(0, nc.scalar.copy)
        weight_cols = place("weight_cols", [P, BLOCKS], F32, 36864)
        nc.vector.tensor_tensor(weight_cols[:], weight_ps[:, :, LAST], sides[:], ALU.mult)
        shift = place("shift", [P, BLOCKS], F32, 36864 + 64)
        nc.vector.tensor_scalar(shift[:], cols_ps[:, THR_ROWS], top_ps[:, LAST:P], None, ALU.subtract)
        weights = psum.tile([P, S], F32, name="weights")
        for b in range(BLOCKS):
            nc.tensor.transpose(weights[:, b * P : (b + 1) * P], weight_cols[:, b : b + 1].to_broadcast([P, P]), ident[:])


        def finish(b, pieces):
            acc = psum.tile([P, S], F32, name=f"acc{b}")
            for o in range(PASSES):
                nc.tensor.matmul_mx(
                    out=acc[:],
                    lhsT=codes[b][:, o].bitcast(FP8X4),
                    lhsT_scale=scales[b][:, o],
                    rhs=picked_words[o][:].bitcast(FP8X4),
                    rhs_scale=picked_scales[4 * o : P, :],
                    start=(o == 0),
                    stop=(o == PASSES - 1),
                )
            base = work.tile([P, S], F32, name="base")
            nc.scalar.activation(base[:], acc[:], ACT.Exp, bias=shift[:, b : b + 1], scale=0.8)
            ex = work.tile([P, 2, S], F32, name="ex")
            total = work.tile([P, 2], F32, name="total")
            denom = work.tile([P, 2], F32, name="denom")
            if b == 1:
                signed = work.tile([P, S], F32, name="signed")
                nc.vector.tensor_tensor(signed[:], weights[:], base[:], ALU.mult)
                for g in range(2):
                    nc.scalar.activation(
                        ex[:, g], signed[:], ACT.Relu, scale=1.0 - 2.0 * g, accum_out=total[:, g : g + 1]
                    )
                nc.vector.tensor_scalar(denom[:], total[:], 0.05, 1.0, ALU.mult, ALU.add)
            else:
                for g, side in enumerate((ALU.max, ALU.min)):
                    nc.vector.scalar_tensor_tensor(
                        ex[:, g], weights[:], 0.0, base[:], side, ALU.mult, accum_out=total[:, g : g + 1]
                    )
                nc.vector.scalar_tensor_tensor(denom[:], total[:], 0.05, ones[:], ALU.mult, ALU.add)
            factor = work.tile([P, 2], F32, name="factor")
            nc.vector.reciprocal(factor[:], denom[:])
            other = work.tile([P, S], F32, name="other")
            result = keep.tile([P, S], F32, name=f"result{b}")
            width = S // pieces
            for c in range(0, S, width):
                cols = slice(c, c + width)
                nc.scalar.activation(other[:, cols], ex[:, 1, cols], ACT.Copy, scale=factor[:, 1:2])
                nc.vector.scalar_tensor_tensor(
                    result[:, cols], ex[:, 0, cols], factor[:, 0:1], other[:, cols], ALU.mult, ALU.subtract
                )
                nc.sync.dma_start(out=out[b * P : (b + 1) * P, cols], in_=result[:, cols])

        quantize(0)
        picked_words.append(place("picked_words1", [P, S], U32, 47040))
        nc.vector.tensor_copy(picked_words[1][:], word_table1[:].bitcast(U32).indirect(offsets[:]))
        prepare(1, nc.vector.tensor_copy)
        finish(0, 1)
        prepare(2, gpsimd_copy)
        finish(1, 1)
        prepare(3, gpsimd_copy)
        finish(2, 1)
        finish(3, 2)
